import numpy as np
import ml_dtypes


def mxq(x, axis, fmt="e4m3"):
    dtype, down = {"e4m3": (ml_dtypes.float8_e4m3fn, 7), "e5m2": (ml_dtypes.float8_e5m2, 14)}[fmt]
    v = np.moveaxis(np.asarray(x, np.float32).astype(ml_dtypes.bfloat16).astype(np.float64), axis, -1)
    blocks = v.reshape(v.shape[:-1] + (-1, 32))
    amax = np.abs(blocks).max(-1, keepdims=True)
    byte = np.maximum(np.where(amax > 0, np.frexp(amax)[1] - 1 + 127, 0) - down, 1)
    scale = np.exp2(byte - 127.0)
    codes = (blocks / scale).astype(np.float32).astype(dtype).astype(np.float64)
    return np.moveaxis((codes * scale).reshape(v.shape), -1, axis)


WIDE = False


def mx_kscale(k):
    if not WIDE:
        return np.ones(k)
    levels = np.array([10, -10, 5, -5, 0])
    if k % 512:
        return np.exp2(np.random.permutation(np.resize(levels, k // 32))).repeat(32)
    a = np.empty((k // 512, 16))
    for p in range(k // 512):
        a[p, :8] = np.random.permutation(np.resize(levels, 8))
        for g in range(8):
            far = levels[np.abs(levels - a[p, g]) >= 10]
            a[p, g + 8] = far[np.random.randint(len(far))]
    return np.exp2(a.ravel()).repeat(32)


def f64(x):
    return np.asarray(x).astype(np.float64)


def striped(idx):
    return np.tile(idx.reshape(-1, 16).T, (8, 1)).astype(np.uint16)


def unstriped(offs):
    return offs[:16].T.reshape(-1).astype(np.int64)


E2M1 = np.array([0.0, 0.5, 1.0, 1.5, 2.0, 3.0, 4.0, 6.0, -0.0, -0.5, -1.0, -1.5, -2.0, -3.0, -4.0, -6.0])


def pack_weight(w, fmt):
    k, n = w.shape
    w = f64(np.asarray(w, np.float32).astype(ml_dtypes.bfloat16)).reshape(k // 32, 32, n)
    amax = np.abs(w).max(1)
    if fmt == "e4m3":
        byte = np.frexp(amax)[1] - 1 + 127 - 7
    else:
        mant, ex = np.frexp(amax / 6.0)
        byte = np.where(mant > 0.5, ex, ex - 1) + 127
    byte = np.clip(np.where(amax > 0, byte, 1), 1, 254)
    scaled = (w * np.exp2(127.0 - byte)[:, None, :]).reshape(k, n).astype(np.float32)
    by_word = np.ascontiguousarray(scaled.reshape(k // 512, 128, 4, n).transpose(0, 1, 3, 2))
    if fmt == "e4m3":
        words = by_word.astype(ml_dtypes.float8_e4m3fn).view(np.uint8)
    else:
        c = by_word.astype(ml_dtypes.float4_e2m1fn).view(np.uint8) & 0xF
        words = (c[..., 0::2] | (c[..., 1::2] << 4)).reshape(k // 512, 128, 2 * n)
    return np.ascontiguousarray(words), np.ascontiguousarray(byte.astype(np.uint8).reshape(k // 512, 16, n))


def unpack_weight(words, scales, fmt):
    g, _, n = scales.shape
    words = np.ascontiguousarray(words).reshape(g, 128, n, -1)
    if fmt == "e4m3":
        vals = words.view(ml_dtypes.float8_e4m3fn).astype(np.float64)
    else:
        nib = np.empty((g, 128, n, 4), np.uint8)
        nib[..., 0::2] = words & 0xF
        nib[..., 1::2] = words >> 4
        vals = E2M1[nib]
    vals = vals * np.repeat(np.exp2(scales.astype(np.float64) - 127.0), 8, axis=1)[..., None]
    return vals.transpose(0, 1, 3, 2).reshape(g * 512, n)


def gelu(v):
    return 0.5 * v * (1.0 + np.tanh(np.sqrt(2.0 / np.pi) * (v + 0.044715 * v**3)))


T, S, K, M, H, N = 2048, 1024, 1024, 512, 1024, 512

def setup_inputs():
    n = np.random.standard_normal
    s = mx_kscale(K)[:, None]
    s2 = mx_kscale(M)[:, None]
    s3 = mx_kscale(M)[:, None]
    u = mx_kscale(H)[:, None]
    tab_words, tab_scales = pack_weight(n((K, T)) * s, "e4m3")
    tab2_words, tab2_scales = pack_weight(n((M, T)) * s2, "e4m3")
    tab3_words, tab3_scales = pack_weight(n((M, T)) * s3, "e2m1")
    wt_words, wt_scales = pack_weight(0.7 * n((K, H)) / np.sqrt(K) / s, "e2m1")
    wd_words, wd_scales = pack_weight(n((M, N)) / np.sqrt(M) / s3, "e4m3")
    return {
        "tab_words": tab_words, "tab_scales": tab_scales,
        "tab2_words": tab2_words, "tab2_scales": tab2_scales,
        "tab3_words": tab3_words, "tab3_scales": tab3_scales,
        "offs": striped(np.random.permutation(T)[:S]),
        "offs2": striped(np.random.permutation(T)[:S]),
        "offs3": striped(np.random.permutation(T)[:S]),
        "wt_words": wt_words, "wt_scales": wt_scales,
        "ws": (0.7 * n((M, H)) / np.sqrt(M) / s2).astype(np.float32),
        "gain": (np.exp(0.3 * n(H)) * u[:, 0]).astype(np.float32),
        "wo": (2.0 * n((H, N)) / np.sqrt(H) / u).astype(np.float32),
        "wd_words": wd_words, "wd_scales": wd_scales,
        "bd": (0.5 * n(N)).astype(np.float32),
    }

def reference(tab_words, tab_scales, tab2_words, tab2_scales, tab3_words, tab3_scales, offs, offs2, offs3,
              wt_words, wt_scales, ws, gain, wo, wd_words, wd_scales, bd):
    v = unpack_weight(tab_words, tab_scales, "e4m3")[:, unstriped(offs)]
    v2 = unpack_weight(tab2_words, tab2_scales, "e4m3")[:, unstriped(offs2)]
    v3 = unpack_weight(tab3_words, tab3_scales, "e2m1")[:, unstriped(offs3)]
    wt = unpack_weight(wt_words, wt_scales, "e2m1")
    wd = unpack_weight(wd_words, wd_scales, "e4m3")
    h = np.tanh(wt.T @ v + mxq(f64(ws), 0, "e4m3").T @ v2) * f64(gain)[:, None]
    y = mxq(f64(wo), 0, "e4m3").T @ mxq(h, 0, "e4m3")
    d = (wd.T @ v3) + f64(bd)[:, None]
    return y * (1.0 / (1.0 + np.exp(-d)))

@@ -1,0 +1,358 @@
+from contextlib import ExitStack
+
+import concourse.mybir as mybir
+from concourse.masks import make_identity
+
+T, S, K, M, H, N = 2048, 1024, 1024, 512, 1024, 512
+FLOPS = 2 * S * (K * H + M * H + H * N + M * N)
+
+F32 = mybir.dt.float32
+BF16 = mybir.dt.bfloat16
+I32 = mybir.dt.int32
+U32 = mybir.dt.uint32
+U16 = mybir.dt.uint16
+U8 = mybir.dt.uint8
+FP8X4 = mybir.dt.float8_e4m3fn_x4
+FP4X4 = mybir.dt.float4_e2m1fn_x4
+ACT = mybir.ActivationFunctionType
+MULT = mybir.AluOpType.mult
+
+P = 128
+HALF = S // 2
+QUARTER = S // 4
+LIST_HALF = HALF // 16
+
+
+def tile_list_patent_gloss_features_kernel(
+    tc, tab_words, tab_scales, tab2_words, tab2_scales, tab3_words, tab3_scales, offs, offs2, offs3,
+    wt_words, wt_scales, ws, gain, wo, wd_words, wd_scales, bd, out,
+):
+    nc = tc.nc
+    with ExitStack() as ctx:
+        keep = ctx.enter_context(tc.tile_pool(name="keep", bufs=1))
+        ring = ctx.enter_context(tc.tile_pool(name="ring", bufs=4))
+        psum = ctx.enter_context(tc.psum_pool(name="psum", bufs=8))
+
+        def held(name, shape, dtype):
+            return keep.tile(shape, dtype, name=name, align_bytes=64)
+
+        def zero(engine, tile):
+            engine.memset(tile[:].bitcast(I32), 0)
+
+        def load_plane(queue, plane, rows):
+            for q in range(4):
+                queue.dma_start(out=plane[32 * q : 32 * q + 4, :].bitcast(I32), in_=rows[4 * q : 4 * q + 4, :].bitcast(I32))
+
+        def gather(dst, window, offsets):
+            nc.vector.tensor_copy(out=dst, in_=window.indirect(offsets))
+
+        def load_words(dst, words):
+            nc.sync.dma_start(out=dst[:], in_=words.rearrange("p t i -> p (t i)").bitcast(I32))
+
+        def quantise(codes, plane, values):
+            nc.vector.quantize_mx(out=codes.bitcast(FP8X4), scales=plane, in_=values)
+
+        def list_half(offsets, h):
+            return offsets[:, h * LIST_HALF : (h + 1) * LIST_HALF]
+
+        list1 = held("list1", [P, S // 16], U16)
+        list2 = held("list2", [P, S // 16], U16)
+        list3 = held("list3", [P, S // 16], U16)
+        tab_plane = held("tab_plane", [P, T], U8)
+        tab2_plane = held("tab2_plane", [P, T], U8)
+        tab3_plane = held("tab3_plane", [P, T], U8)
+        wt_plane_raw = held("wt_plane_raw", [P, 2 * H], U8)
+        wd_plane = held("wd_plane", [P, N], U8)
+        v_plane1 = held("v_plane1", [P, S], U8)
+        bias_rows = held("bias_rows", [P, P], F32)
+        gain_rows = held("gain_rows", [P, P], F32)
+        ident = held("ident", [P, P], F32)
+        warm = held("warm", [P, 1], F32)
+
+        def shared(tag, name, shape, dtype):
+            return keep.tile(shape, dtype, name=name, tag=tag, align_bytes=64)
+
+        for plane in (tab3_plane, tab_plane):
+            nc.vector.memset(plane[:, 0 : T // 2].bitcast(I32), 0)
+            nc.gpsimd.memset(plane[:, T // 2 : T].bitcast(I32), 0)
+        zero(nc.vector, wd_plane)
+        zero(nc.vector, tab2_plane)
+        zero(nc.vector, wt_plane_raw)
+        zero(nc.vector, v_plane1)
+        nc.vector.memset(gain_rows[:], 0.0)
+        nc.gpsimd.memset(bias_rows[:], 0.0)
+        nc.gpsimd.dma_start(out=bias_rows[0:4, :], in_=bd.rearrange("(c p) -> c p", p=P))
+        make_identity(nc, ident[:])
+        for q in range(4):
+            nc.gpsimd.dma_start(
+                out=wt_plane_raw[32 * q : 32 * q + 4, :].bitcast(I32).rearrange("r (a c) -> r a c", a=2),
+                in_=wt_scales[:, 4 * q : 4 * q + 4, :].bitcast(I32).rearrange("a r c -> r a c"),
+            )
+        for b in range(2):
+            nc.gpsimd.dma_start(
+                out=gain_rows[4 * b : 4 * b + 4, :].rearrange("t (g i) -> t g i", i=8),
+                in_=gain[512 * b : 512 * (b + 1)].rearrange("(g t i) -> t g i", t=4, i=8),
+            )
+        nc.scalar.activation(out=warm[:], in_=ident[:, 0:1], func=ACT.Sigmoid)
+
+        tab3_win = shared("tab3_then_tab1", "tab3_win", [P, T // 2], I32)
+        tab_win = [held("tab_win0", [P, T], I32)]
+        wt_raw = shared("wt_then_tab2", "wt_raw", [P, 2, H // 2], I32)
+        wd_codes = held("wd_codes", [P, N], I32)
+
+        def load_ws(b):
+            raw = shared("ws_raw", "ws_raw", [P, 4, 512], F32)
+            nc.sync.dma_start(out=raw[:], in_=ws[:, 512 * b : 512 * (b + 1)].rearrange("(p j) c -> p j c", j=4))
+            return raw
+
+        nc.sync.dma_start(list3[:], offs3)
+        nc.sync.dma_start(list1[:], offs)
+        nc.sync.dma_start(list2[:], offs2)
+        load_plane(nc.sync, tab3_plane, tab3_scales[0])
+        nc.sync.dma_start(out=tab3_win[:], in_=tab3_words[0].bitcast(I32))
+        load_words(tab_win[0], tab_words[0])
+        for q in range(4):
+            nc.sync.dma_start(out=tab_plane[32 * q : 32 * q + 8, :].bitcast(I32), in_=tab_scales[:, 4 * q : 4 * q + 4, :].bitcast(I32))
+        load_words(wd_codes, wd_words[0])
+        nc.sync.dma_start(out=wt_raw[:], in_=wt_words.rearrange("a p c -> p a c").bitcast(I32))
+        load_plane(nc.sync, wd_plane, wd_scales[0])
+        ws_raw = [load_ws(0)]
+        load_plane(nc.sync, tab2_plane, tab2_scales[0])
+
+        v3_plane = held("v3_plane", [P, S], U8)
+        v3_codes = [held(f"v3_codes{h}", [P, 2 * HALF], U8) for h in range(2)]
+        v_plane0 = held("v_plane0", [P, S], U8)
+        v_plane = [v_plane0, v_plane1]
+        v_codes = [[held(f"v_codes{a}{h}", [P, HALF], U32) for h in range(2)] for a in range(2)]
+        v2_plane = [held(f"v2_plane{h}", [P, HALF], U8) for h in range(2)]
+        v2_codes = [held(f"v2_codes{h}", [P, HALF], U32) for h in range(2)]
+        ws_codes = [held(f"ws_codes{b}", [P, 512], U32) for b in range(2)]
+        ws_plane = [held(f"ws_plane{b}", [P, 512], U8) for b in range(2)]
+        ws_bf = [shared("ws_bf_then_wo", "ws_bf0", [P, 4, 512], BF16), held("ws_bf1", [P, 4, 512], BF16)]
+        wo_codes = [held(f"wo_codes{b}", [P, N], U32) for b in range(2)]
+        wo_plane = [held(f"wo_plane{b}", [P, N], U8) for b in range(2)]
+        wo_bf = [held(f"wo_bf{b}", [P, N, 4], BF16) for b in range(2)]
+        wt_codes = held("wt_codes", [P, H], I32)
+        wt_plane = held("wt_plane", [P, 2 * H], U8)
+        h_codes = [[held(f"h_codes{b}{q}", [P, QUARTER], U32) for q in range(4)] for b in range(2)]
+        h_plane = [[held(f"h_plane{b}{q}", [P, QUARTER], U8) for q in range(4)] for b in range(2)]
+        gate = [held(f"gate{h}", [P, 4, HALF], F32) for h in range(2)]
+        bias = held("bias", [P, 4], F32)
+        gains = held("gains", [P, 8], F32)
+
+        def new_bank():
+            return psum.tile([P, 512], F32, name="bank")
+
+        def gather_v(a, h):
+            gather(v_codes[a][h][:], tab_win[a][:].bitcast(U32), list_half(list1, h))
+
+        def gather_v2_plane(h):
+            gather(v2_plane[h][:], tab2_plane[:], list_half(list2, h))
+
+        def gather_v2(h):
+            gather(v2_codes[h][:], tab2_win[:].bitcast(U32), list_half(list2, h))
+
+        def cast_ws(b):
+            src = ws_raw[b][:].rearrange("p j (g t u i) -> p t g u j i", t=4, u=2, i=4)
+            dst = ws_bf[b][:].rearrange("p t (g u i j) -> p t g u j i", u=2, i=4, j=4)
+            for t in range(4):
+                nc.scalar.copy(out=dst[:, t], in_=src[:, t])
+
+        def quantise_ws(b):
+            quantise(ws_codes[b][:], ws_plane[b][:], ws_bf[b][:].rearrange("p t c -> p (t c)"))
+
+        def cast_wo(b):
+            nc.scalar.copy(
+                out=wo_bf[b][:].rearrange("p (c i) t -> p c t i", i=4),
+                in_=wo_raw[:, b].rearrange("p t (c i) -> p c t i", i=4),
+            )
+
+        def quantise_wo(b):
+            quantise(wo_codes[b][:], wo_plane[b][:], wo_bf[b][:].rearrange("p n t -> p (n t)"))
+
+        def domain(h):
+            for c in range(4):
+                bank = new_bank()
+                nc.tensor.matmul_mx(
+                    out=bank[:],
+                    lhsT=wd_codes[:, c * P : (c + 1) * P].bitcast(FP8X4),
+                    lhsT_scale=wd_plane[:, c * P : (c + 1) * P],
+                    rhs=v3_codes[h][:].bitcast(FP4X4),
+                    rhs_scale=v3_plane[:, h * HALF : (h + 1) * HALF],
+                    start=True,
+                    stop=True,
+                )
+                nc.scalar.activation(out=gate[h][:, c, :], in_=bank[:], func=ACT.Sigmoid, bias=bias[:, c : c + 1])
+
+        def token_pass(bank, a, b, e):
+            h, r = divmod(e, 4)
+            for t in range(4):
+                c0 = (2 * a + b) * 512 + t * P
+                nc.tensor.matmul_mx(
+                    out=bank[:, t * P : (t + 1) * P],
+                    lhsT=wt_codes[:, c0 // 2 : (c0 + P) // 2].bitcast(FP4X4),
+                    lhsT_scale=wt_plane[:, c0 : c0 + P],
+                    rhs=v_codes[a][h][:, r * P : (r + 1) * P].bitcast(FP8X4),
+                    rhs_scale=v_plane[a][:, e * P : (e + 1) * P],
+                    start=(a == 0 and t == 0),
+                    stop=False,
+                )
+
+        def sense_pass(bank, b, e):
+            h, r = divmod(e, 4)
+            for t in range(4):
+                nc.tensor.matmul_mx(
+                    out=bank[:, t * P : (t + 1) * P],
+                    lhsT=ws_codes[b][:, t * P : (t + 1) * P].bitcast(FP8X4),
+                    lhsT_scale=ws_plane[b][:, t * P : (t + 1) * P],
+                    rhs=v2_codes[h][:, r * P : (r + 1) * P].bitcast(FP8X4),
+                    rhs_scale=v2_plane[h][:, r * P : (r + 1) * P],
+                    start=False,
+                    stop=(t == 3),
+                )
+
+        def finish_unit(banks, b, q):
+            th = ring.tile([P, QUARTER, 4], F32, name="th")
+            for u in range(2):
+                sense_pass(banks[u], b, 2 * q + u)
+                nc.scalar.activation(
+                    out=th[:, u * P : (u + 1) * P, :], in_=banks[u][:].rearrange("p (t j) -> p j t", t=4), func=ACT.Tanh
+                )
+            return th
+
+        def whole_unit(b, q):
+            th = ring.tile([P, QUARTER, 4], F32, name="th")
+            for u in range(2):
+                bank = new_bank()
+                for a in range(2):
+                    token_pass(bank, a, b, 2 * q + u)
+                sense_pass(bank, b, 2 * q + u)
+                nc.scalar.activation(
+                    out=th[:, u * P : (u + 1) * P, :], in_=bank[:].rearrange("p (t j) -> p j t", t=4), func=ACT.Tanh
+                )
+            return th
+
+        def apply_gain(th, b):
+            hb = ring.tile([P, QUARTER, 4], BF16, name="hb", align_bytes=64)
+            g = gains[:, 4 * b : 4 * b + 4].unsqueeze(1).to_broadcast([P, QUARTER, 4])
+            nc.vector.tensor_tensor(out=hb[:], in0=th[:], in1=g, op=MULT)
+            return hb
+
+        def quantise_h(hb, b, q):
+            quantise(h_codes[b][q][:], h_plane[b][q][:], hb[:].rearrange("p j t -> p (j t)"))
+
+        def outputs(q):
+            h, r = divmod(q, 2)
+            for pair in range(2):
+                bank = new_bank()
+                for u in range(2):
+                    c = 2 * pair + u
+                    for b in range(2):
+                        nc.tensor.matmul_mx(
+                            out=bank[:, u * QUARTER : (u + 1) * QUARTER],
+                            lhsT=wo_codes[b][:, c * P : (c + 1) * P].bitcast(FP8X4),
+                            lhsT_scale=wo_plane[b][:, c * P : (c + 1) * P],
+                            rhs=h_codes[b][q][:].bitcast(FP8X4),
+                            rhs_scale=h_plane[b][q][:],
+                            start=(b == 0),
+                            stop=(b == 1),
+                        )
+                res = ring.tile([P, 2, QUARTER], F32, name="res")
+                nc.vector.tensor_tensor(
+                    out=res[:],
+                    in0=bank[:].rearrange("p (u j) -> p u j", u=2),
+                    in1=gate[h][:, 2 * pair : 2 * pair + 2, r * QUARTER : (r + 1) * QUARTER],
+                    op=MULT,
+                )
+                nc.sync.dma_start(
+                    out=out[2 * pair * P : (2 * pair + 2) * P, q * QUARTER : (q + 1) * QUARTER].rearrange("(u p) j -> p u j", p=P),
+                    in_=res[:],
+                )
+
+        def rows_to_partitions(dst, rows):
+            bank = new_bank()
+            nc.tensor.transpose(bank[:, 0:P], rows[:], ident[:])
+            nc.scalar.copy(out=dst[:], in_=bank[:, 0 : dst.shape[1]])
+
+        rows_to_partitions(bias, bias_rows)
+
+        gather(v3_plane[:], tab3_plane[:], list3[:])
+        for h in range(2):
+            gather(v3_codes[h][:].bitcast(U16), tab3_win[:].bitcast(U16), list_half(list3, h))
+        tab_win.append(shared("tab3_then_tab1", "tab_win1", [P, T], I32))
+        load_words(tab_win[1], tab_words[1])
+        gather(v_plane0[:], tab_plane[:], list1[:])
+        for q in range(4):
+            nc.sync.dma_start(out=v_plane1[32 * q : 32 * q + 4, :].bitcast(I32), in_=v_plane0[32 * q + 4 : 32 * q + 8, :].bitcast(I32))
+        domain(0)
+        nc.vector.tensor_copy(
+            out=wt_codes[:].rearrange("p (c t g w) -> p c t g w", t=4, g=16, w=4),
+            in_=wt_raw[:].rearrange("p a (b g t w) -> p (a b) t g w", b=2, g=16, t=4),
+        )
+        tab2_win = shared("wt_then_tab2", "tab2_win", [P, T], I32)
+        load_words(tab2_win, tab2_words[0])
+        gather_v(0, 0)
+        nc.vector.tensor_copy(
+            out=wt_plane[:].bitcast(I32).rearrange("p (c t g w) -> p c t g w", t=4, g=16, w=2),
+            in_=wt_plane_raw[:].bitcast(I32).rearrange("p (c g t w) -> p c t g w", g=16, t=4, w=2),
+        )
+        cast_ws(0)
+        ws_raw.append(load_ws(1))
+        domain(1)
+        rows_to_partitions(gains, gain_rows)
+        gather_v(1, 0)
+        gather_v2_plane(0)
+        quantise_ws(0)
+        wo_raw = shared("ws_bf_then_wo", "wo_raw", [P, 2, 4, N], F32)
+        for b in range(2):
+            wo_b = wo[512 * b : 512 * (b + 1), :].rearrange("(g t i) n -> t g i n", t=4, i=8)
+            for t in range(4):
+                nc.sync.dma_start(out=wo_raw[:, b, t, :], in_=wo_b[t])
+        gather_v2(0)
+
+        banks = [[new_bank() for e in range(4)] for b in range(2)]
+        for b in range(2):
+            for e in range(4):
+                token_pass(banks[b][e], 0, b, e)
+        for e in range(4):
+            token_pass(banks[0][e], 1, 0, e)
+        th00 = finish_unit(banks[0][0:2], 0, 0)
+        gather_v(0, 1)
+        gather_v(1, 1)
+        cast_ws(1)
+        th01 = finish_unit(banks[0][2:4], 0, 1)
+        for e in range(4):
+            token_pass(banks[1][e], 1, 1, e)
+        quantise_ws(1)
+        gather_v2_plane(1)
+        gather_v2(1)
+        th10 = finish_unit(banks[1][0:2], 1, 0)
+        th11 = finish_unit(banks[1][2:4], 1, 1)
+        hb00 = apply_gain(th00, 0)
+        cast_wo(0)
+        hb01 = apply_gain(th01, 0)
+        quantise_h(hb00, 0, 0)
+        th02 = whole_unit(0, 2)
+        hb10 = apply_gain(th10, 1)
+        quantise_h(hb01, 0, 1)
+        cast_wo(1)
+        quantise_wo(0)
+        hb11 = apply_gain(th11, 1)
+        quantise_h(hb10, 1, 0)
+        th12 = whole_unit(1, 2)
+        quantise_wo(1)
+        hb02 = apply_gain(th02, 0)
+        quantise_h(hb11, 1, 1)
+        th03 = whole_unit(0, 3)
+        outputs(0)
+        quantise_h(hb02, 0, 2)
+        hb12 = apply_gain(th12, 1)
+        th13 = whole_unit(1, 3)
+        outputs(1)
+        quantise_h(hb12, 1, 2)
+        hb03 = apply_gain(th03, 0)
+        hb13 = apply_gain(th13, 1)
+        quantise_h(hb03, 0, 3)
+        outputs(2)
+        quantise_h(hb13, 1, 3)
+        outputs(3)

@@ -59,45 +59,34 @@ def tile_list_patent_gloss_features_kernel(
         list2 = held("list2", [P, S // 16], U16)
         list3 = held("list3", [P, S // 16], U16)
         tab_plane = held("tab_plane", [P, T], U8)
-        tab2_plane = held("tab2_plane", [P, T], U8)
         tab3_plane = held("tab3_plane", [P, T], U8)
         wt_plane_raw = held("wt_plane_raw", [P, 2 * H], U8)
         wd_plane = held("wd_plane", [P, N], U8)
         v_plane1 = held("v_plane1", [P, S], U8)
-        bias_rows = held("bias_rows", [P, P], F32)
-        gain_rows = held("gain_rows", [P, P], F32)
+        const_rows = held("const_rows", [P, 2 * P], F32)
         ident = held("ident", [P, P], F32)
         warm = held("warm", [P, 1], F32)
 
         def shared(tag, name, shape, dtype):
             return keep.tile(shape, dtype, name=name, tag=tag, align_bytes=64)
 
+        tab2_plane = held("tab2_plane", [P, T], U8)
         for plane in (tab3_plane, tab_plane):
             nc.vector.memset(plane[:, 0 : T // 2].bitcast(I32), 0)
             nc.gpsimd.memset(plane[:, T // 2 : T].bitcast(I32), 0)
-        zero(nc.vector, wd_plane)
-        zero(nc.vector, tab2_plane)
         zero(nc.vector, wt_plane_raw)
+        zero(nc.vector, tab2_plane)
         zero(nc.vector, v_plane1)
-        nc.vector.memset(gain_rows[:], 0.0)
-        nc.gpsimd.memset(bias_rows[:], 0.0)
-        nc.gpsimd.dma_start(out=bias_rows[0:4, :], in_=bd.rearrange("(c p) -> c p", p=P))
+        nc.vector.memset(warm[:], 0.0)
+        nc.scalar.activation(out=warm[:], in_=warm[:], func=ACT.Sigmoid)
+        zero(nc.gpsimd, wd_plane)
+        nc.gpsimd.memset(const_rows[:], 0.0)
         make_identity(nc, ident[:])
-        for q in range(4):
-            nc.gpsimd.dma_start(
-                out=wt_plane_raw[32 * q : 32 * q + 4, :].bitcast(I32).rearrange("r (a c) -> r a c", a=2),
-                in_=wt_scales[:, 4 * q : 4 * q + 4, :].bitcast(I32).rearrange("a r c -> r a c"),
-            )
-        for b in range(2):
-            nc.gpsimd.dma_start(
-                out=gain_rows[4 * b : 4 * b + 4, :].rearrange("t (g i) -> t g i", i=8),
-                in_=gain[512 * b : 512 * (b + 1)].rearrange("(g t i) -> t g i", t=4, i=8),
-            )
-        nc.scalar.activation(out=warm[:], in_=ident[:, 0:1], func=ACT.Sigmoid)
 
-        tab3_win = shared("tab3_then_tab1", "tab3_win", [P, T // 2], I32)
-        tab_win = [held("tab_win0", [P, T], I32)]
-        wt_raw = shared("wt_then_tab2", "wt_raw", [P, 2, H // 2], I32)
+        tab3_win = held("tab3_win", [P, T // 2], I32)
+        tab_win = [held(f"tab_win{a}", [P, T], I32) for a in range(2)]
+        tab2_win = shared("tab2_then_v", "tab2_win", [P, T], I32)
+        wt_raw = held("wt_raw", [P, 2, H // 2], I32)
         wd_codes = held("wd_codes", [P, N], I32)
 
         def load_ws(b):
@@ -110,21 +99,36 @@ def tile_list_patent_gloss_features_kernel(
         nc.sync.dma_start(list2[:], offs2)
         load_plane(nc.sync, tab3_plane, tab3_scales[0])
         nc.sync.dma_start(out=tab3_win[:], in_=tab3_words[0].bitcast(I32))
-        load_words(tab_win[0], tab_words[0])
-        for q in range(4):
-            nc.sync.dma_start(out=tab_plane[32 * q : 32 * q + 8, :].bitcast(I32), in_=tab_scales[:, 4 * q : 4 * q + 4, :].bitcast(I32))
+        ws_raw = [load_ws(0)]
+        tab_rows = tab_scales.bitcast(I32).rearrange("a (q r) w -> r q a w", r=4)
+        for r in range(4):
+            nc.sync.dma_start(out=tab_plane[r:P:16, :].bitcast(I32), in_=tab_rows[r])
         load_words(wd_codes, wd_words[0])
         nc.sync.dma_start(out=wt_raw[:], in_=wt_words.rearrange("a p c -> p a c").bitcast(I32))
         load_plane(nc.sync, wd_plane, wd_scales[0])
-        ws_raw = [load_ws(0)]
-        load_plane(nc.sync, tab2_plane, tab2_scales[0])
+        nc.sync.dma_start(out=const_rows[4:8, 0:P], in_=bd.rearrange("(c p) -> c p", p=P))
+        nc.sync.dma_start(
+            out=const_rows[0:4, :].rearrange("t (g i) -> t g i", i=8), in_=gain.rearrange("(g t i) -> t g i", t=4, i=8)
+        )
+        load_words(tab_win[0], tab_words[0])
+        for q in range(4):
+            nc.sync.dma_start(
+                out=wt_plane_raw[32 * q : 32 * q + 4, :].bitcast(I32).rearrange("r (a c) -> r a c", a=2),
+                in_=wt_scales[:, 4 * q : 4 * q + 4, :].bitcast(I32).rearrange("a r c -> r a c"),
+            )
+        load_words(tab_win[1], tab_words[1])
+        for q in range(4):
+            nc.sync.dma_start(
+                out=tab2_plane[32 * q + 4 : 32 * q + 8, :].bitcast(I32), in_=tab2_scales[0, 4 * q : 4 * q + 4, :].bitcast(I32)
+            )
+        load_words(tab2_win, tab2_words[0])
 
         v3_plane = held("v3_plane", [P, S], U8)
         v3_codes = [held(f"v3_codes{h}", [P, 2 * HALF], U8) for h in range(2)]
         v_plane0 = held("v_plane0", [P, S], U8)
         v_plane = [v_plane0, v_plane1]
-        v_codes = [[held(f"v_codes{a}{h}", [P, HALF], U32) for h in range(2)] for a in range(2)]
-        v2_plane = [held(f"v2_plane{h}", [P, HALF], U8) for h in range(2)]
+        v_codes = [[held(f"v_codes{a}0", [P, HALF], U32)[:]] for a in range(2)]
+        v2_plane = held("v2_plane", [P, S], U8)
         v2_codes = [held(f"v2_codes{h}", [P, HALF], U32) for h in range(2)]
         ws_codes = [held(f"ws_codes{b}", [P, 512], U32) for b in range(2)]
         ws_plane = [held(f"ws_plane{b}", [P, 512], U8) for b in range(2)]
@@ -137,17 +141,13 @@ def tile_list_patent_gloss_features_kernel(
         h_codes = [[held(f"h_codes{b}{q}", [P, QUARTER], U32) for q in range(4)] for b in range(2)]
         h_plane = [[held(f"h_plane{b}{q}", [P, QUARTER], U8) for q in range(4)] for b in range(2)]
         gate = [held(f"gate{h}", [P, 4, HALF], F32) for h in range(2)]
-        bias = held("bias", [P, 4], F32)
-        gains = held("gains", [P, 8], F32)
+        consts = held("consts", [P, 2, 8], F32)
 
         def new_bank():
             return psum.tile([P, 512], F32, name="bank")
 
         def gather_v(a, h):
-            gather(v_codes[a][h][:], tab_win[a][:].bitcast(U32), list_half(list1, h))
-
-        def gather_v2_plane(h):
-            gather(v2_plane[h][:], tab2_plane[:], list_half(list2, h))
+            gather(v_codes[a][h], tab_win[a][:].bitcast(U32), list_half(list1, h))
 
         def gather_v2(h):
             gather(v2_codes[h][:], tab2_win[:].bitcast(U32), list_half(list2, h))
@@ -182,7 +182,7 @@ def tile_list_patent_gloss_features_kernel(
                     start=True,
                     stop=True,
                 )
-                nc.scalar.activation(out=gate[h][:, c, :], in_=bank[:], func=ACT.Sigmoid, bias=bias[:, c : c + 1])
+                nc.scalar.activation(out=gate[h][:, c, :], in_=bank[:], func=ACT.Sigmoid, bias=consts[:, 0, 4 + c : 5 + c])
 
         def token_pass(bank, a, b, e):
             h, r = divmod(e, 4)
@@ -206,7 +206,7 @@ def tile_list_patent_gloss_features_kernel(
                     lhsT=ws_codes[b][:, t * P : (t + 1) * P].bitcast(FP8X4),
                     lhsT_scale=ws_plane[b][:, t * P : (t + 1) * P],
                     rhs=v2_codes[h][:, r * P : (r + 1) * P].bitcast(FP8X4),
-                    rhs_scale=v2_plane[h][:, r * P : (r + 1) * P],
+                    rhs_scale=v2_plane[4:P, e * P : (e + 1) * P],
                     start=False,
                     stop=(t == 3),
                 )
@@ -234,7 +234,7 @@ def tile_list_patent_gloss_features_kernel(
 
         def apply_gain(th, b):
             hb = ring.tile([P, QUARTER, 4], BF16, name="hb", align_bytes=64)
-            g = gains[:, 4 * b : 4 * b + 4].unsqueeze(1).to_broadcast([P, QUARTER, 4])
+            g = consts[:, b, 0:4].unsqueeze(1).to_broadcast([P, QUARTER, 4])
             nc.vector.tensor_tensor(out=hb[:], in0=th[:], in1=g, op=MULT)
             return hb
 
@@ -269,46 +269,65 @@ def tile_list_patent_gloss_features_kernel(
                     in_=res[:],
                 )
 
-        def rows_to_partitions(dst, rows):
-            bank = new_bank()
-            nc.tensor.transpose(bank[:, 0:P], rows[:], ident[:])
-            nc.scalar.copy(out=dst[:], in_=bank[:, 0 : dst.shape[1]])
+        def scalar_unit(b, q):
+            th = ring.tile([P, 4, QUARTER], F32, name="th")
+            for u in range(2):
+                bank = new_bank()
+                for a in range(2):
+                    token_pass(bank, a, b, 2 * q + u)
+                sense_pass(bank, b, 2 * q + u)
+                nc.scalar.activation(
+                    out=th[:, :, u * P : (u + 1) * P], in_=bank[:].rearrange("p (t j) -> p t j", t=4), func=ACT.Tanh
+                )
+            return th
 
-        rows_to_partitions(bias, bias_rows)
+        def scalar_gain(th, b):
+            rows = held("gain_rows_bf", [P, 4, QUARTER], BF16)
+            for t in range(4):
+                nc.scalar.activation(out=rows[:, t, :], in_=th[:, t, :], func=ACT.Copy, scale=consts[:, b, t : t + 1])
+            hb = ring.tile([P, QUARTER, 4], BF16, name="hb", align_bytes=64)
+            nc.scalar.copy(
+                out=hb[:].rearrange("p (c i) t -> p c t i", i=4), in_=rows[:].rearrange("p t (c i) -> p c t i", i=4)
+            )
+            return hb
+
+        cast_ws(0)
+        const_bank = new_bank()
+        for b in range(2):
+            nc.tensor.transpose(const_bank[:, b * P : (b + 1) * P], const_rows[:, b * P : (b + 1) * P], ident[:])
+        nc.scalar.copy(out=consts[:], in_=const_bank[:, 0 : 2 * P].rearrange("p (b c) -> p b c", b=2)[:, :, 0:8])
 
         gather(v3_plane[:], tab3_plane[:], list3[:])
         for h in range(2):
             gather(v3_codes[h][:].bitcast(U16), tab3_win[:].bitcast(U16), list_half(list3, h))
-        tab_win.append(shared("tab3_then_tab1", "tab_win1", [P, T], I32))
-        load_words(tab_win[1], tab_words[1])
         gather(v_plane0[:], tab_plane[:], list1[:])
         for q in range(4):
-            nc.sync.dma_start(out=v_plane1[32 * q : 32 * q + 4, :].bitcast(I32), in_=v_plane0[32 * q + 4 : 32 * q + 8, :].bitcast(I32))
+            nc.sync.dma_start(out=v_plane1[32 * q : 32 * q + 4, :].bitcast(I32), in_=v_plane0[32 * q + 16 : 32 * q + 20, :].bitcast(I32))
+        ws_raw.append(load_ws(1))
         domain(0)
+        gather_v(0, 0)
         nc.vector.tensor_copy(
             out=wt_codes[:].rearrange("p (c t g w) -> p c t g w", t=4, g=16, w=4),
             in_=wt_raw[:].rearrange("p a (b g t w) -> p (a b) t g w", b=2, g=16, t=4),
         )
-        tab2_win = shared("wt_then_tab2", "tab2_win", [P, T], I32)
-        load_words(tab2_win, tab2_words[0])
-        gather_v(0, 0)
         nc.vector.tensor_copy(
             out=wt_plane[:].bitcast(I32).rearrange("p (c t g w) -> p c t g w", t=4, g=16, w=2),
             in_=wt_plane_raw[:].bitcast(I32).rearrange("p (c g t w) -> p c t g w", g=16, t=4, w=2),
         )
-        cast_ws(0)
-        ws_raw.append(load_ws(1))
         domain(1)
-        rows_to_partitions(gains, gain_rows)
         gather_v(1, 0)
-        gather_v2_plane(0)
         quantise_ws(0)
         wo_raw = shared("ws_bf_then_wo", "wo_raw", [P, 2, 4, N], F32)
         for b in range(2):
             wo_b = wo[512 * b : 512 * (b + 1), :].rearrange("(g t i) n -> t g i n", t=4, i=8)
             for t in range(4):
                 nc.sync.dma_start(out=wo_raw[:, b, t, :], in_=wo_b[t])
+        gather(v2_plane[:], tab2_plane[:], list2[:])
         gather_v2(0)
+        gather_v2(1)
+        v_second = shared("tab2_then_v", "v_second", [P, 2, HALF], U32)
+        for a in range(2):
+            v_codes[a].append(v_second[:, a, :])
 
         banks = [[new_bank() for e in range(4)] for b in range(2)]
         for b in range(2):
@@ -316,16 +335,14 @@ def tile_list_patent_gloss_features_kernel(
                 token_pass(banks[b][e], 0, b, e)
         for e in range(4):
             token_pass(banks[0][e], 1, 0, e)
+        cast_ws(1)
         th00 = finish_unit(banks[0][0:2], 0, 0)
         gather_v(0, 1)
+        quantise_ws(1)
         gather_v(1, 1)
-        cast_ws(1)
         th01 = finish_unit(banks[0][2:4], 0, 1)
         for e in range(4):
             token_pass(banks[1][e], 1, 1, e)
-        quantise_ws(1)
-        gather_v2_plane(1)
-        gather_v2(1)
         th10 = finish_unit(banks[1][0:2], 1, 0)
         th11 = finish_unit(banks[1][2:4], 1, 1)
         hb00 = apply_gain(th00, 0)
@@ -343,16 +360,16 @@ def tile_list_patent_gloss_features_kernel(
         quantise_wo(1)
         hb02 = apply_gain(th02, 0)
         quantise_h(hb11, 1, 1)
-        th03 = whole_unit(0, 3)
+        th03 = scalar_unit(0, 3)
         outputs(0)
         quantise_h(hb02, 0, 2)
         hb12 = apply_gain(th12, 1)
         th13 = whole_unit(1, 3)
+        hb03 = scalar_gain(th03, 0)
         outputs(1)
         quantise_h(hb12, 1, 2)
-        hb03 = apply_gain(th03, 0)
         hb13 = apply_gain(th13, 1)
-        quantise_h(hb03, 0, 3)
         outputs(2)
         quantise_h(hb13, 1, 3)
+        quantise_h(hb03, 0, 3)
         outputs(3)

@@ -241,26 +241,30 @@ def tile_list_patent_gloss_features_kernel(
         def quantise_h(hb, b, q):
             quantise(h_codes[b][q][:], h_plane[b][q][:], hb[:].rearrange("p j t -> p (j t)"))
 
-        def outputs(q):
+        def output_pass(bank, pair, b, q, first):
+            for u in range(2):
+                c = 2 * pair + u
+                nc.tensor.matmul_mx(
+                    out=bank[:, u * QUARTER : (u + 1) * QUARTER],
+                    lhsT=wo_codes[b][:, c * P : (c + 1) * P].bitcast(FP8X4),
+                    lhsT_scale=wo_plane[b][:, c * P : (c + 1) * P],
+                    rhs=h_codes[b][q][:].bitcast(FP8X4),
+                    rhs_scale=h_plane[b][q][:],
+                    start=(first and u == 0),
+                    stop=(not first and u == 1),
+                )
+
+        def outputs(q, early):
             h, r = divmod(q, 2)
+            banks = [new_bank() for pair in range(2)]
             for pair in range(2):
-                bank = new_bank()
-                for u in range(2):
-                    c = 2 * pair + u
-                    for b in range(2):
-                        nc.tensor.matmul_mx(
-                            out=bank[:, u * QUARTER : (u + 1) * QUARTER],
-                            lhsT=wo_codes[b][:, c * P : (c + 1) * P].bitcast(FP8X4),
-                            lhsT_scale=wo_plane[b][:, c * P : (c + 1) * P],
-                            rhs=h_codes[b][q][:].bitcast(FP8X4),
-                            rhs_scale=h_plane[b][q][:],
-                            start=(b == 0),
-                            stop=(b == 1),
-                        )
+                output_pass(banks[pair], pair, early, q, True)
+            for pair in range(2):
+                output_pass(banks[pair], pair, 1 - early, q, False)
                 res = ring.tile([P, 2, QUARTER], F32, name="res")
                 nc.vector.tensor_tensor(
                     out=res[:],
-                    in0=bank[:].rearrange("p (u j) -> p u j", u=2),
+                    in0=banks[pair][:].rearrange("p (u j) -> p u j", u=2),
                     in1=gate[h][:, 2 * pair : 2 * pair + 2, r * QUARTER : (r + 1) * QUARTER],
                     op=MULT,
                 )
@@ -361,15 +365,15 @@ def tile_list_patent_gloss_features_kernel(
         hb02 = apply_gain(th02, 0)
         quantise_h(hb11, 1, 1)
         th03 = scalar_unit(0, 3)
-        outputs(0)
+        outputs(0, 0)
         quantise_h(hb02, 0, 2)
         hb12 = apply_gain(th12, 1)
         th13 = whole_unit(1, 3)
         hb03 = scalar_gain(th03, 0)
-        outputs(1)
+        outputs(1, 0)
         quantise_h(hb12, 1, 2)
         hb13 = apply_gain(th13, 1)
-        outputs(2)
+        outputs(2, 0)
         quantise_h(hb13, 1, 3)
         quantise_h(hb03, 0, 3)
-        outputs(3)
+        outputs(3, 1)

from contextlib import ExitStack

import concourse.mybir as mybir
from concourse.masks import make_identity

T, S, K, M, H, N = 2048, 1024, 1024, 512, 1024, 512
FLOPS = 2 * S * (K * H + M * H + H * N + M * N)

F32 = mybir.dt.float32
BF16 = mybir.dt.bfloat16
I32 = mybir.dt.int32
U32 = mybir.dt.uint32
U16 = mybir.dt.uint16
U8 = mybir.dt.uint8
FP8X4 = mybir.dt.float8_e4m3fn_x4
FP4X4 = mybir.dt.float4_e2m1fn_x4
ACT = mybir.ActivationFunctionType
MULT = mybir.AluOpType.mult

P = 128
HALF = S // 2
QUARTER = S // 4
LIST_HALF = HALF // 16


def tile_list_patent_gloss_features_kernel(
    tc, tab_words, tab_scales, tab2_words, tab2_scales, tab3_words, tab3_scales, offs, offs2, offs3,
    wt_words, wt_scales, ws, gain, wo, wd_words, wd_scales, bd, out,
):
    nc = tc.nc
    with ExitStack() as ctx:
        keep = ctx.enter_context(tc.tile_pool(name="keep", bufs=1))
        ring = ctx.enter_context(tc.tile_pool(name="ring", bufs=4))
        psum = ctx.enter_context(tc.psum_pool(name="psum", bufs=8))

        def held(name, shape, dtype):
            return keep.tile(shape, dtype, name=name, align_bytes=64)

        def zero(engine, tile):
            engine.memset(tile[:].bitcast(I32), 0)

        def load_plane(queue, plane, rows):
            for q in range(4):
                queue.dma_start(out=plane[32 * q : 32 * q + 4, :].bitcast(I32), in_=rows[4 * q : 4 * q + 4, :].bitcast(I32))

        def gather(dst, window, offsets):
            nc.vector.tensor_copy(out=dst, in_=window.indirect(offsets))

        def load_words(dst, words):
            nc.sync.dma_start(out=dst[:], in_=words.rearrange("p t i -> p (t i)").bitcast(I32))

        def quantise(codes, plane, values):
            nc.vector.quantize_mx(out=codes.bitcast(FP8X4), scales=plane, in_=values)

        def list_half(offsets, h):
            return offsets[:, h * LIST_HALF : (h + 1) * LIST_HALF]

        list1 = held("list1", [P, S // 16], U16)
        list2 = held("list2", [P, S // 16], U16)
        list3 = held("list3", [P, S // 16], U16)
        tab_plane = held("tab_plane", [P, T], U8)
        tab3_plane = held("tab3_plane", [P, T], U8)
        wt_plane_raw = held("wt_plane_raw", [P, 2 * H], U8)
        wd_plane = held("wd_plane", [P, N], U8)
        v_plane1 = held("v_plane1", [P, S], U8)
        const_rows = held("const_rows", [P, 2 * P], F32)
        ident = held("ident", [P, P], F32)
        warm = held("warm", [P, 1], F32)

        def shared(tag, name, shape, dtype):
            return keep.tile(shape, dtype, name=name, tag=tag, align_bytes=64)

        tab2_plane = held("tab2_plane", [P, T], U8)
        for plane in (tab3_plane, tab_plane):
            nc.vector.memset(plane[:, 0 : T // 2].bitcast(I32), 0)
            nc.gpsimd.memset(plane[:, T // 2 : T].bitcast(I32), 0)
        zero(nc.vector, wt_plane_raw)
        zero(nc.vector, tab2_plane)
        zero(nc.vector, v_plane1)
        nc.vector.memset(warm[:], 0.0)
        nc.scalar.activation(out=warm[:], in_=warm[:], func=ACT.Sigmoid)
        zero(nc.gpsimd, wd_plane)
        nc.gpsimd.memset(const_rows[:], 0.0)
        make_identity(nc, ident[:])

        tab3_win = held("tab3_win", [P, T // 2], I32)
        tab_win = [held(f"tab_win{a}", [P, T], I32) for a in range(2)]
        tab2_win = shared("tab2_then_v", "tab2_win", [P, T], I32)
        wt_raw = held("wt_raw", [P, 2, H // 2], I32)
        wd_codes = held("wd_codes", [P, N], I32)

        def load_ws(b):
            raw = shared("ws_raw", "ws_raw", [P, 4, 512], F32)
            nc.sync.dma_start(out=raw[:], in_=ws[:, 512 * b : 512 * (b + 1)].rearrange("(p j) c -> p j c", j=4))
            return raw

        nc.sync.dma_start(list3[:], offs3)
        nc.sync.dma_start(list1[:], offs)
        nc.sync.dma_start(list2[:], offs2)
        load_plane(nc.sync, tab3_plane, tab3_scales[0])
        nc.sync.dma_start(out=tab3_win[:], in_=tab3_words[0].bitcast(I32))
        ws_raw = [load_ws(0)]
        tab_rows = tab_scales.bitcast(I32).rearrange("a (q r) w -> r q a w", r=4)
        for r in range(4):
            nc.sync.dma_start(out=tab_plane[r:P:16, :].bitcast(I32), in_=tab_rows[r])
        load_words(wd_codes, wd_words[0])
        nc.sync.dma_start(out=wt_raw[:], in_=wt_words.rearrange("a p c -> p a c").bitcast(I32))
        load_plane(nc.sync, wd_plane, wd_scales[0])
        nc.sync.dma_start(out=const_rows[4:8, 0:P], in_=bd.rearrange("(c p) -> c p", p=P))
        nc.sync.dma_start(
            out=const_rows[0:4, :].rearrange("t (g i) -> t g i", i=8), in_=gain.rearrange("(g t i) -> t g i", t=4, i=8)
        )
        load_words(tab_win[0], tab_words[0])
        for q in range(4):
            nc.sync.dma_start(
                out=wt_plane_raw[32 * q : 32 * q + 4, :].bitcast(I32).rearrange("r (a c) -> r a c", a=2),
                in_=wt_scales[:, 4 * q : 4 * q + 4, :].bitcast(I32).rearrange("a r c -> r a c"),
            )
        load_words(tab_win[1], tab_words[1])
        for q in range(4):
            nc.sync.dma_start(
                out=tab2_plane[32 * q + 4 : 32 * q + 8, :].bitcast(I32), in_=tab2_scales[0, 4 * q : 4 * q + 4, :].bitcast(I32)
            )
        load_words(tab2_win, tab2_words[0])

        v3_plane = held("v3_plane", [P, S], U8)
        v3_codes = [held(f"v3_codes{h}", [P, 2 * HALF], U8) for h in range(2)]
        v_plane0 = held("v_plane0", [P, S], U8)
        v_plane = [v_plane0, v_plane1]
        v_codes = [[held(f"v_codes{a}0", [P, HALF], U32)[:]] for a in range(2)]
        v2_plane = held("v2_plane", [P, S], U8)
        v2_codes = [held(f"v2_codes{h}", [P, HALF], U32) for h in range(2)]
        ws_codes = [held(f"ws_codes{b}", [P, 512], U32) for b in range(2)]
        ws_plane = [held(f"ws_plane{b}", [P, 512], U8) for b in range(2)]
        ws_bf = [shared("ws_bf_then_wo", "ws_bf0", [P, 4, 512], BF16), held("ws_bf1", [P, 4, 512], BF16)]
        wo_codes = [held(f"wo_codes{b}", [P, N], U32) for b in range(2)]
        wo_plane = [held(f"wo_plane{b}", [P, N], U8) for b in range(2)]
        wo_bf = [held(f"wo_bf{b}", [P, N, 4], BF16) for b in range(2)]
        wt_codes = held("wt_codes", [P, H], I32)
        wt_plane = held("wt_plane", [P, 2 * H], U8)
        h_codes = [[held(f"h_codes{b}{q}", [P, QUARTER], U32) for q in range(4)] for b in range(2)]
        h_plane = [[held(f"h_plane{b}{q}", [P, QUARTER], U8) for q in range(4)] for b in range(2)]
        gate = [held(f"gate{h}", [P, 4, HALF], F32) for h in range(2)]
        consts = held("consts", [P, 2, 8], F32)

        def new_bank():
            return psum.tile([P, 512], F32, name="bank")

        def gather_v(a, h):
            gather(v_codes[a][h], tab_win[a][:].bitcast(U32), list_half(list1, h))

        def gather_v2(h):
            gather(v2_codes[h][:], tab2_win[:].bitcast(U32), list_half(list2, h))

        def cast_ws(b):
            src = ws_raw[b][:].rearrange("p j (g t u i) -> p t g u j i", t=4, u=2, i=4)
            dst = ws_bf[b][:].rearrange("p t (g u i j) -> p t g u j i", u=2, i=4, j=4)
            for t in range(4):
                nc.scalar.copy(out=dst[:, t], in_=src[:, t])

        def quantise_ws(b):
            quantise(ws_codes[b][:], ws_plane[b][:], ws_bf[b][:].rearrange("p t c -> p (t c)"))

        def cast_wo(b):
            nc.scalar.copy(
                out=wo_bf[b][:].rearrange("p (c i) t -> p c t i", i=4),
                in_=wo_raw[:, b].rearrange("p t (c i) -> p c t i", i=4),
            )

        def quantise_wo(b):
            quantise(wo_codes[b][:], wo_plane[b][:], wo_bf[b][:].rearrange("p n t -> p (n t)"))

        def domain(h):
            for c in range(4):
                bank = new_bank()
                nc.tensor.matmul_mx(
                    out=bank[:],
                    lhsT=wd_codes[:, c * P : (c + 1) * P].bitcast(FP8X4),
                    lhsT_scale=wd_plane[:, c * P : (c + 1) * P],
                    rhs=v3_codes[h][:].bitcast(FP4X4),
                    rhs_scale=v3_plane[:, h * HALF : (h + 1) * HALF],
                    start=True,
                    stop=True,
                )
                nc.scalar.activation(out=gate[h][:, c, :], in_=bank[:], func=ACT.Sigmoid, bias=consts[:, 0, 4 + c : 5 + c])

        def token_pass(bank, a, b, e):
            h, r = divmod(e, 4)
            for t in range(4):
                c0 = (2 * a + b) * 512 + t * P
                nc.tensor.matmul_mx(
                    out=bank[:, t * P : (t + 1) * P],
                    lhsT=wt_codes[:, c0 // 2 : (c0 + P) // 2].bitcast(FP4X4),
                    lhsT_scale=wt_plane[:, c0 : c0 + P],
                    rhs=v_codes[a][h][:, r * P : (r + 1) * P].bitcast(FP8X4),
                    rhs_scale=v_plane[a][:, e * P : (e + 1) * P],
                    start=(a == 0 and t == 0),
                    stop=False,
                )

        def sense_pass(bank, b, e):
            h, r = divmod(e, 4)
            for t in range(4):
                nc.tensor.matmul_mx(
                    out=bank[:, t * P : (t + 1) * P],
                    lhsT=ws_codes[b][:, t * P : (t + 1) * P].bitcast(FP8X4),
                    lhsT_scale=ws_plane[b][:, t * P : (t + 1) * P],
                    rhs=v2_codes[h][:, r * P : (r + 1) * P].bitcast(FP8X4),
                    rhs_scale=v2_plane[4:P, e * P : (e + 1) * P],
                    start=False,
                    stop=(t == 3),
                )

        def finish_unit(banks, b, q):
            th = ring.tile([P, QUARTER, 4], F32, name="th")
            for u in range(2):
                sense_pass(banks[u], b, 2 * q + u)
                nc.scalar.activation(
                    out=th[:, u * P : (u + 1) * P, :], in_=banks[u][:].rearrange("p (t j) -> p j t", t=4), func=ACT.Tanh
                )
            return th

        def whole_unit(b, q):
            th = ring.tile([P, QUARTER, 4], F32, name="th")
            for u in range(2):
                bank = new_bank()
                for a in range(2):
                    token_pass(bank, a, b, 2 * q + u)
                sense_pass(bank, b, 2 * q + u)
                nc.scalar.activation(
                    out=th[:, u * P : (u + 1) * P, :], in_=bank[:].rearrange("p (t j) -> p j t", t=4), func=ACT.Tanh
                )
            return th

        def apply_gain(th, b):
            hb = ring.tile([P, QUARTER, 4], BF16, name="hb", align_bytes=64)
            g = consts[:, b, 0:4].unsqueeze(1).to_broadcast([P, QUARTER, 4])
            nc.vector.tensor_tensor(out=hb[:], in0=th[:], in1=g, op=MULT)
            return hb

        def quantise_h(hb, b, q):
            quantise(h_codes[b][q][:], h_plane[b][q][:], hb[:].rearrange("p j t -> p (j t)"))

        def output_pass(bank, pair, b, q, first):
            for u in range(2):
                c = 2 * pair + u
                nc.tensor.matmul_mx(
                    out=bank[:, u * QUARTER : (u + 1) * QUARTER],
                    lhsT=wo_codes[b][:, c * P : (c + 1) * P].bitcast(FP8X4),
                    lhsT_scale=wo_plane[b][:, c * P : (c + 1) * P],
                    rhs=h_codes[b][q][:].bitcast(FP8X4),
                    rhs_scale=h_plane[b][q][:],
                    start=(first and u == 0),
                    stop=(not first and u == 1),
                )

        def outputs(q, early):
            h, r = divmod(q, 2)
            banks = [new_bank() for pair in range(2)]
            for pair in range(2):
                output_pass(banks[pair], pair, early, q, True)
            for pair in range(2):
                output_pass(banks[pair], pair, 1 - early, q, False)
                res = ring.tile([P, 2, QUARTER], F32, name="res")
                nc.vector.tensor_tensor(
                    out=res[:],
                    in0=banks[pair][:].rearrange("p (u j) -> p u j", u=2),
                    in1=gate[h][:, 2 * pair : 2 * pair + 2, r * QUARTER : (r + 1) * QUARTER],
                    op=MULT,
                )
                nc.sync.dma_start(
                    out=out[2 * pair * P : (2 * pair + 2) * P, q * QUARTER : (q + 1) * QUARTER].rearrange("(u p) j -> p u j", p=P),
                    in_=res[:],
                )

        def scalar_unit(b, q):
            th = ring.tile([P, 4, QUARTER], F32, name="th")
            for u in range(2):
                bank = new_bank()
                for a in range(2):
                    token_pass(bank, a, b, 2 * q + u)
                sense_pass(bank, b, 2 * q + u)
                nc.scalar.activation(
                    out=th[:, :, u * P : (u + 1) * P], in_=bank[:].rearrange("p (t j) -> p t j", t=4), func=ACT.Tanh
                )
            return th

        def scalar_gain(th, b):
            rows = held("gain_rows_bf", [P, 4, QUARTER], BF16)
            for t in range(4):
                nc.scalar.activation(out=rows[:, t, :], in_=th[:, t, :], func=ACT.Copy, scale=consts[:, b, t : t + 1])
            hb = ring.tile([P, QUARTER, 4], BF16, name="hb", align_bytes=64)
            nc.scalar.copy(
                out=hb[:].rearrange("p (c i) t -> p c t i", i=4), in_=rows[:].rearrange("p t (c i) -> p c t i", i=4)
            )
            return hb

        cast_ws(0)
        const_bank = new_bank()
        for b in range(2):
            nc.tensor.transpose(const_bank[:, b * P : (b + 1) * P], const_rows[:, b * P : (b + 1) * P], ident[:])
        nc.scalar.copy(out=consts[:], in_=const_bank[:, 0 : 2 * P].rearrange("p (b c) -> p b c", b=2)[:, :, 0:8])

        gather(v3_plane[:], tab3_plane[:], list3[:])
        for h in range(2):
            gather(v3_codes[h][:].bitcast(U16), tab3_win[:].bitcast(U16), list_half(list3, h))
        gather(v_plane0[:], tab_plane[:], list1[:])
        for q in range(4):
            nc.sync.dma_start(out=v_plane1[32 * q : 32 * q + 4, :].bitcast(I32), in_=v_plane0[32 * q + 16 : 32 * q + 20, :].bitcast(I32))
        ws_raw.append(load_ws(1))
        domain(0)
        gather_v(0, 0)
        nc.vector.tensor_copy(
            out=wt_codes[:].rearrange("p (c t g w) -> p c t g w", t=4, g=16, w=4),
            in_=wt_raw[:].rearrange("p a (b g t w) -> p (a b) t g w", b=2, g=16, t=4),
        )
        nc.vector.tensor_copy(
            out=wt_plane[:].bitcast(I32).rearrange("p (c t g w) -> p c t g w", t=4, g=16, w=2),
            in_=wt_plane_raw[:].bitcast(I32).rearrange("p (c g t w) -> p c t g w", g=16, t=4, w=2),
        )
        domain(1)
        gather_v(1, 0)
        quantise_ws(0)
        wo_raw = shared("ws_bf_then_wo", "wo_raw", [P, 2, 4, N], F32)
        for b in range(2):
            wo_b = wo[512 * b : 512 * (b + 1), :].rearrange("(g t i) n -> t g i n", t=4, i=8)
            for t in range(4):
                nc.sync.dma_start(out=wo_raw[:, b, t, :], in_=wo_b[t])
        gather(v2_plane[:], tab2_plane[:], list2[:])
        gather_v2(0)
        gather_v2(1)
        v_second = shared("tab2_then_v", "v_second", [P, 2, HALF], U32)
        for a in range(2):
            v_codes[a].append(v_second[:, a, :])

        banks = [[new_bank() for e in range(4)] for b in range(2)]
        for b in range(2):
            for e in range(4):
                token_pass(banks[b][e], 0, b, e)
        for e in range(4):
            token_pass(banks[0][e], 1, 0, e)
        cast_ws(1)
        th00 = finish_unit(banks[0][0:2], 0, 0)
        gather_v(0, 1)
        quantise_ws(1)
        gather_v(1, 1)
        th01 = finish_unit(banks[0][2:4], 0, 1)
        for e in range(4):
            token_pass(banks[1][e], 1, 1, e)
        th10 = finish_unit(banks[1][0:2], 1, 0)
        th11 = finish_unit(banks[1][2:4], 1, 1)
        hb00 = apply_gain(th00, 0)
        cast_wo(0)
        hb01 = apply_gain(th01, 0)
        quantise_h(hb00, 0, 0)
        th02 = whole_unit(0, 2)
        hb10 = apply_gain(th10, 1)
        quantise_h(hb01, 0, 1)
        cast_wo(1)
        quantise_wo(0)
        hb11 = apply_gain(th11, 1)
        quantise_h(hb10, 1, 0)
        th12 = whole_unit(1, 2)
        quantise_wo(1)
        hb02 = apply_gain(th02, 0)
        quantise_h(hb11, 1, 1)
        th03 = scalar_unit(0, 3)
        outputs(0, 0)
        quantise_h(hb02, 0, 2)
        hb12 = apply_gain(th12, 1)
        th13 = whole_unit(1, 3)
        hb03 = scalar_gain(th03, 0)
        outputs(1, 0)
        quantise_h(hb12, 1, 2)
        hb13 = apply_gain(th13, 1)
        outputs(2, 0)
        quantise_h(hb13, 1, 3)
        quantise_h(hb03, 0, 3)
        outputs(3, 1)
